import numpy as np
import ml_dtypes


def mxq(x, axis, fmt="e4m3"):
    dtype, down = {"e4m3": (ml_dtypes.float8_e4m3fn, 7), "e5m2": (ml_dtypes.float8_e5m2, 14)}[fmt]
    v = np.moveaxis(np.asarray(x, np.float32).astype(ml_dtypes.bfloat16).astype(np.float64), axis, -1)
    blocks = v.reshape(v.shape[:-1] + (-1, 32))
    amax = np.abs(blocks).max(-1, keepdims=True)
    byte = np.maximum(np.where(amax > 0, np.frexp(amax)[1] - 1 + 127, 0) - down, 1)
    scale = np.exp2(byte - 127.0)
    codes = (blocks / scale).astype(np.float32).astype(dtype).astype(np.float64)
    return np.moveaxis((codes * scale).reshape(v.shape), -1, axis)


WIDE = False


def mx_kscale(k):
    if not WIDE:
        return np.ones(k)
    levels = np.array([10, -10, 5, -5, 0])
    if k % 512:
        return np.exp2(np.random.permutation(np.resize(levels, k // 32))).repeat(32)
    a = np.empty((k // 512, 16))
    for p in range(k // 512):
        a[p, :8] = np.random.permutation(np.resize(levels, 8))
        for g in range(8):
            far = levels[np.abs(levels - a[p, g]) >= 10]
            a[p, g + 8] = far[np.random.randint(len(far))]
    return np.exp2(a.ravel()).repeat(32)


def f64(x):
    return np.asarray(x).astype(np.float64)


def striped(idx):
    return np.tile(idx.reshape(-1, 16).T, (8, 1)).astype(np.uint16)


def unstriped(offs):
    return offs[:16].T.reshape(-1).astype(np.int64)


def gelu(v):
    return 0.5 * v * (1.0 + np.tanh(np.sqrt(2.0 / np.pi) * (v + 0.044715 * v**3)))


K, T, E, C, H, N = 2560, 512, 2, 256, 512, 512


def by_expert(wq, xq):
    return np.concatenate([wq[e].T @ xq[:, e * C:(e + 1) * C] for e in range(E)], axis=1)


def setup_inputs():
    n = np.random.standard_normal
    s = mx_kscale(K)[:, None]
    u = mx_kscale(H)
    return {
        "xT": (n((K, T)) * s).astype(np.float32),
        "w1": (n((E, K, H)) / np.sqrt(K) / s[None]).astype(np.float32),
        "w3": (n((E, K, H)) / np.sqrt(K) / s[None] * u[None, None, :]).astype(np.float32),
        "w2": (n((E, H, N)) / np.sqrt(H) / u[None, :, None]).astype(np.float32),
        "gate": np.tile(np.random.uniform(0.2, 1.0, E * C), (N, 1)).astype(np.float32),
        "offs": striped(np.random.permutation(T)[:E * C]),
        "dst": striped(np.random.permutation(T)[:E * C]),
    }


def reference(xT, w1, w3, w2, gate, offs, dst):
    idx = unstriped(offs)
    xq = mxq(f64(xT)[:, idx], 0, "e4m3")
    h = gelu(by_expert(mxq(f64(w1), 1, "e4m3"), xq))
    h = h * by_expert(mxq(f64(w3), 1, "e4m3"), xq)
    y = by_expert(mxq(f64(w2), 1, "e4m3"), mxq(h, 0, "e4m3"))
    out = np.zeros((N, T))
    out[:, unstriped(dst)] = f64(gate) * y
    return out

@@ -1,0 +1,186 @@
+from contextlib import ExitStack
+
+import concourse.mybir as mybir
+
+K, T, E, C, H, N = 2560, 512, 2, 256, 512, 512
+P = 128
+PACK = 4
+K_PASS = P * PACK
+PASSES = K // K_PASS
+TILES = H // P
+LIST_COLS = C // 16
+
+FLOPS = 2 * E * C * (2 * K * H + H * N)
+BYTES = 4 * (K * T + 2 * E * K * H + E * H * N + E * C + N * T) + 2 * 2 * P * E * LIST_COLS
+
+F32 = mybir.dt.float32
+BF16 = mybir.dt.bfloat16
+U32 = mybir.dt.uint32
+U16 = mybir.dt.uint16
+U8 = mybir.dt.uint8
+FP8X4 = mybir.dt.float8_e4m3fn_x4
+GELU = mybir.ActivationFunctionType.Gelu_apprx_tanh
+MULT = mybir.AluOpType.mult
+
+SCALAR_GROUPS = 96
+
+
+def tile_moe_two_glu_gelu_kernel(tc, xT, w1, w3, w2, gate, offs, dst, out):
+    nc = tc.nc
+    with ExitStack() as ctx:
+        keep = ctx.enter_context(tc.tile_pool(name="keep", bufs=1))
+        stage = ctx.enter_context(tc.tile_pool(name="stage", bufs=10))
+        mid = ctx.enter_context(tc.tile_pool(name="mid", bufs=4))
+        work = ctx.enter_context(tc.tile_pool(name="work", bufs=2))
+        psum = ctx.enter_context(tc.psum_pool(name="psum", bufs=8))
+
+        offs_list = keep.tile([P, E * LIST_COLS], U16, name="offs_list")
+        dst_list = keep.tile([P, E * LIST_COLS], U16, name="dst_list")
+        gate_rows = keep.tile([P, E * C], F32, name="gate_rows")
+        warm = keep.tile([P, 8], F32, name="warm")
+        nc.vector.memset(warm[:], 0.0)
+        nc.scalar.activation(warm[:], warm[:], GELU)
+
+        token_words, token_bytes = [], []
+        for s in range(PASSES):
+            words = keep.tile([P, T], U32, name=f"token_words{s}", align_bytes=64)
+            scales = keep.tile([P, T], U8, name=f"token_bytes{s}", align_bytes=64)
+            nc.gpsimd.memset(scales[:], 0)
+            token_words.append(words)
+            token_bytes.append(scales)
+        slot_words = {}
+        slot_bytes = {}
+        for e in range(E):
+            for s in range(PASSES):
+                slot_words[e, s] = keep.tile([P, C], U32, name=f"slot_words{e}{s}", align_bytes=64)
+                slot_bytes[e, s] = keep.tile([P, C], U8, name=f"slot_bytes{e}{s}", align_bytes=64)
+        placed = [keep.tile([P, T], F32, name=f"placed{n}") for n in range(N // P)]
+
+        def load(rows):
+            raw = stage.tile([P, PACK, 512], F32, name="raw")
+            nc.sync.dma_start(out=raw[:], in_=rows.rearrange("(p j) w -> p j w", j=PACK))
+            return raw
+
+        def group(raw, permuted, cut=SCALAR_GROUPS):
+            grouped = mid.tile([P, PACK * 512], BF16, name="grouped", align_bytes=64)
+            if permuted:
+                target = grouped[:].rearrange("p (t m j) -> p m j t", t=4, j=PACK)
+            else:
+                target = grouped[:].rearrange("p (m t j) -> p m j t", t=4, j=PACK)
+            source = raw[:].rearrange("p j (m t) -> p m j t", t=4)
+            nc.scalar.copy(target[:, 0:cut], source[:, 0:cut])
+            nc.vector.tensor_copy(target[:, cut:P], source[:, cut:P])
+            return grouped
+
+        def quantise(grouped, words, scales, pieces=1):
+            width = 512 // pieces
+            for q in range(pieces):
+                cols = slice(q * width, (q + 1) * width)
+                nc.vector.quantize_mx(
+                    out=words[:, cols].bitcast(FP8X4),
+                    scales=scales[:, cols],
+                    in_=grouped[:, q * width * PACK : (q + 1) * width * PACK],
+                )
+
+        def weight(rows, permuted, name, cut=SCALAR_GROUPS, pieces=1):
+            raw = load(rows)
+            grouped = group(raw, permuted, cut)
+            words = keep.tile([P, 512], U32, name=f"{name}_words", align_bytes=64)
+            scales = keep.tile([P, 512], U8, name=f"{name}_bytes", align_bytes=64)
+            quantise(grouped, words, scales, pieces)
+            return words, scales
+
+        def tokens(s):
+            raw = load(xT[s * K_PASS : (s + 1) * K_PASS, :])
+            grouped = group(raw, False)
+            quantise(grouped, token_words[s], token_bytes[s])
+
+        def gather(e, s):
+            picks = offs_list[:, e * LIST_COLS : (e + 1) * LIST_COLS]
+            nc.vector.tensor_copy(slot_words[e, s][:], token_words[s][:].indirect(picks))
+            nc.vector.tensor_copy(slot_bytes[e, s][:], token_bytes[s][:].indirect(picks))
+
+        def product(acc, wq, m, words, scales, start, stop):
+            cols = slice(m * P, (m + 1) * P)
+            nc.tensor.matmul_mx(
+                out=acc,
+                lhsT=wq[0][:, cols].bitcast(FP8X4),
+                lhsT_scale=wq[1][:, cols],
+                rhs=words.bitcast(FP8X4),
+                rhs_scale=scales,
+                start=start,
+                stop=stop,
+            )
+
+        def project(e, s, banks, wq):
+            for t in range(TILES):
+                product(banks[t][:, 0:C], wq, t, slot_words[e, s][:], slot_bytes[e, s][:], s == 0, s == PASSES - 1)
+
+        def hidden_rows(w, e, s):
+            return w[e, s * K_PASS : (s + 1) * K_PASS, :]
+
+        def open_banks():
+            banks = []
+            for t in range(TILES):
+                bank = psum.tile([P, 512], F32, name="bank")
+                banks.append(bank)
+            return banks
+
+        def hidden(e, banks_b, activated):
+            product_h = work.tile([P, TILES, C], F32, name="product_h")
+            for t in range(TILES):
+                nc.vector.tensor_tensor(product_h[:, t, :], activated[:, t, :], banks_b[t][:, 0:C], MULT)
+            grouped = work.tile([P, C * PACK], BF16, name="grouped_h", align_bytes=64)
+            target = grouped[:].rearrange("p (c i j) -> p c j i", i=4, j=PACK)
+            source = product_h[:].rearrange("p j (c i) -> p c j i", i=4)
+            cut = 24
+            nc.scalar.copy(target[:, 0:cut], source[:, 0:cut])
+            nc.vector.tensor_copy(target[:, cut : C // 4], source[:, cut : C // 4])
+            words = work.tile([P, C], U32, name="h_words", align_bytes=64)
+            scales = work.tile([P, C], U8, name="h_bytes", align_bytes=64)
+            nc.vector.quantize_mx(out=words[:].bitcast(FP8X4), scales=scales[:], in_=grouped[:])
+            return words, scales
+
+        def place(e, w2q, words, scales):
+            picks = dst_list[:, e * LIST_COLS : (e + 1) * LIST_COLS]
+            ys = []
+            for half in range(2):
+                bank = psum.tile([P, 512], F32, name="bank")
+                for u in range(2):
+                    product(bank[:, u * C : (u + 1) * C], w2q, 2 * half + u, words[:], scales[:], True, True)
+                for u in range(2):
+                    y = work.tile([P, C], F32, name=f"y{2 * half + u}")
+                    nc.vector.tensor_tensor(y[:], bank[:, u * C : (u + 1) * C], gate_rows[:, e * C : (e + 1) * C], MULT)
+                    ys.append(y)
+            for n in range(N // P):
+                nc.vector.tensor_copy(placed[n][:].indirect(picks), ys[n][:])
+
+        for e in range(E):
+            banks_a = open_banks()
+            for s in range(PASSES):
+                if e == 0:
+                    tokens(s)
+                    if s == 0:
+                        nc.sync.dma_start(offs_list[:], offs)
+                w1q = weight(hidden_rows(w1, e, s), True, f"w1_{e}{s}")
+                gather(e, s)
+                project(e, s, banks_a, w1q)
+            activated = work.tile([P, TILES, C], F32, name="activated")
+            for t in range(TILES):
+                nc.scalar.activation(activated[:, t, :], banks_a[t][:, 0:C], GELU)
+            banks_b = open_banks()
+            for s in range(PASSES):
+                last = e == E - 1 and s == PASSES - 1
+                if last:
+                    w3q = weight(hidden_rows(w3, e, s), True, f"w3_{e}{s}", cut=44, pieces=4)
+                else:
+                    w3q = weight(hidden_rows(w3, e, s), True, f"w3_{e}{s}")
+                project(e, s, banks_b, w3q)
+            if e == 0:
+                nc.sync.dma_start(dst_list[:], dst)
+                nc.sync.dma_start(gate_rows[:], gate[0:P, :])
+            w2q = weight(w2[e], False, f"w2_{e}")
+            h_words, h_bytes = hidden(e, banks_b, activated)
+            place(e, w2q, h_words, h_bytes)
+        for n in range(N // P):
+            nc.sync.dma_start(out[n * P : (n + 1) * P, :], placed[n][:])

@@ -1,17 +1,21 @@
 from contextlib import ExitStack
 
 import concourse.mybir as mybir
+from concourse.masks import make_identity
 
 K, T, E, C, H, N = 2560, 512, 2, 256, 512, 512
 P = 128
 PACK = 4
 K_PASS = P * PACK
 PASSES = K // K_PASS
-TILES = H // P
+PLANES = 2
+SLOT_TILES = C // P
 LIST_COLS = C // 16
 
 FLOPS = 2 * E * C * (2 * K * H + H * N)
 BYTES = 4 * (K * T + 2 * E * K * H + E * H * N + E * C + N * T) + 2 * 2 * P * E * LIST_COLS
+
+CFG = {'stage': 10, 'mid': 4, 'lists': 12, 'x0': 2, 'share': [88, 88, 88, 88, 88, 88, 88, 88, 88, 88, 88, 88, 88, 64, 0, 88, 88, 64, 128, 100, 128, 128, 0, 0, 100], 'cut': [64, 30, 64, 64], 'col0': [0], 'col1': [], 'fused': [[0, 1, 0, 1], [1, 1, 1, 1]], 'jobs': [(3, ('gw', 0, 0)), (4, ('gw', 0, 1)), (5, ('gw', 0, 2)), (6, ('gw', 0, 3)), (7, ('gw', 0, 4)), (5, ('gp', 0, 0)), (7, ('gp', 0, 1)), (8, ('gw', 1, 0)), (9, ('gw', 1, 1)), (10, ('gw', 1, 2)), (11, ('gw', 1, 3)), (12, ('gw', 1, 4)), (13, ('gp', 1, 0)), (14, ('gp', 1, 1)), (12, ('gelu', 0, 0)), (16, ('hid', 0, 0)), (17, ('col', 0, 0)), (18, ('qh', 0, 0)), (18, ('down', 0, 0)), (18, ('leave', 0, 0)), (19, ('sc', 0, 0)), (18, ('down', 0, 1)), (18, ('leave', 0, 1)), (19, ('sc', 0, 1)), (18, ('down', 0, 2)), (18, ('leave', 0, 2)), (19, ('sc', 0, 2)), (18, ('down', 0, 3)), (18, ('leave', 0, 3)), (19, ('sc', 0, 3)), (23, ('gelu', 1, 0))], 'stream': [('x', 0, 0), ('x', 0, 1), ('x', 0, 2), ('x', 0, 3), ('x', 0, 4), ('w1', 0, 0), ('w1', 0, 1), ('w1', 0, 2), ('w1', 0, 3), ('w1', 0, 4), ('w3', 0, 0), ('w3', 0, 1), ('w3', 0, 2), ('w3', 0, 3), ('w3', 0, 4), ('w1', 1, 0), ('w2', 0, 2), ('w1', 1, 1), ('w1', 1, 2), ('w1', 1, 3), ('w1', 1, 4), ('w3', 1, 0), ('w3', 1, 1), ('w3', 1, 2), ('w3', 1, 3)]}
 
 F32 = mybir.dt.float32
 BF16 = mybir.dt.bfloat16
@@ -22,15 +26,13 @@ FP8X4 = mybir.dt.float8_e4m3fn_x4
 GELU = mybir.ActivationFunctionType.Gelu_apprx_tanh
 MULT = mybir.AluOpType.mult
 
-SCALAR_GROUPS = 96
-
 
 def tile_moe_two_glu_gelu_kernel(tc, xT, w1, w3, w2, gate, offs, dst, out):
     nc = tc.nc
     with ExitStack() as ctx:
         keep = ctx.enter_context(tc.tile_pool(name="keep", bufs=1))
-        stage = ctx.enter_context(tc.tile_pool(name="stage", bufs=10))
-        mid = ctx.enter_context(tc.tile_pool(name="mid", bufs=4))
+        stage = ctx.enter_context(tc.tile_pool(name="stage", bufs=CFG["stage"]))
+        mid = ctx.enter_context(tc.tile_pool(name="mid", bufs=CFG["mid"]))
         work = ctx.enter_context(tc.tile_pool(name="work", bufs=2))
         psum = ctx.enter_context(tc.psum_pool(name="psum", bufs=8))
 
@@ -40,147 +42,247 @@ def tile_moe_two_glu_gelu_kernel(tc, xT, w1, w3, w2, gate, offs, dst, out):
         warm = keep.tile([P, 8], F32, name="warm")
         nc.vector.memset(warm[:], 0.0)
         nc.scalar.activation(warm[:], warm[:], GELU)
+        identity = keep.tile([P, P], F32, name="identity")
+        make_identity(nc, identity[:])
 
-        token_words, token_bytes = [], []
-        for s in range(PASSES):
-            words = keep.tile([P, T], U32, name=f"token_words{s}", align_bytes=64)
-            scales = keep.tile([P, T], U8, name=f"token_bytes{s}", align_bytes=64)
-            nc.gpsimd.memset(scales[:], 0)
-            token_words.append(words)
-            token_bytes.append(scales)
+        token_words = [keep.tile([P, T], U32, name=f"token_words{s}", align_bytes=64) for s in range(PASSES)]
+        token_planes = [keep.tile([P, T], U8, name=f"token_planes{q}", align_bytes=64) for q in range(PLANES)]
+        for plane in token_planes:
+            nc.gpsimd.memset(plane[:], 0)
         slot_words = {}
-        slot_bytes = {}
+        slot_planes = {}
         for e in range(E):
             for s in range(PASSES):
                 slot_words[e, s] = keep.tile([P, C], U32, name=f"slot_words{e}{s}", align_bytes=64)
-                slot_bytes[e, s] = keep.tile([P, C], U8, name=f"slot_bytes{e}{s}", align_bytes=64)
+            for q in range(PLANES):
+                slot_planes[e, q] = keep.tile([P, C], U8, name=f"slot_planes{e}{q}", align_bytes=64)
         placed = [keep.tile([P, T], F32, name=f"placed{n}") for n in range(N // P)]
 
-        def load(rows):
+        def load(rows, pieces=1):
             raw = stage.tile([P, PACK, 512], F32, name="raw")
-            nc.sync.dma_start(out=raw[:], in_=rows.rearrange("(p j) w -> p j w", j=PACK))
-            return raw
-
-        def group(raw, permuted, cut=SCALAR_GROUPS):
-            grouped = mid.tile([P, PACK * 512], BF16, name="grouped", align_bytes=64)
-            if permuted:
-                target = grouped[:].rearrange("p (t m j) -> p m j t", t=4, j=PACK)
-            else:
-                target = grouped[:].rearrange("p (m t j) -> p m j t", t=4, j=PACK)
-            source = raw[:].rearrange("p j (m t) -> p m j t", t=4)
-            nc.scalar.copy(target[:, 0:cut], source[:, 0:cut])
-            nc.vector.tensor_copy(target[:, cut:P], source[:, cut:P])
-            return grouped
-
-        def quantise(grouped, words, scales, pieces=1):
+            view = rows.rearrange("(p j) w -> p j w", j=PACK)
             width = 512 // pieces
             for q in range(pieces):
                 cols = slice(q * width, (q + 1) * width)
-                nc.vector.quantize_mx(
-                    out=words[:, cols].bitcast(FP8X4),
-                    scales=scales[:, cols],
-                    in_=grouped[:, q * width * PACK : (q + 1) * width * PACK],
-                )
+                nc.sync.dma_start(out=raw[:, :, cols], in_=view[:, :, cols])
+            return raw
 
-        def weight(rows, permuted, name, cut=SCALAR_GROUPS, pieces=1):
-            raw = load(rows)
-            grouped = group(raw, permuted, cut)
-            words = keep.tile([P, 512], U32, name=f"{name}_words", align_bytes=64)
-            scales = keep.tile([P, 512], U8, name=f"{name}_bytes", align_bytes=64)
-            quantise(grouped, words, scales, pieces)
+        def interleave(grouped, raw, first, cut, last):
+            target = grouped[:].rearrange("p (c i j) -> p c j i", i=4, j=PACK)
+            source = raw[:].rearrange("p j (c i) -> p c j i", i=4)
+            if cut > first:
+                nc.scalar.copy(target[:, first:cut], source[:, first:cut])
+            if last > cut:
+                nc.vector.tensor_copy(target[:, cut:last], source[:, cut:last])
+
+        def quantise(codes, grouped, first=0, last=512):
+            nc.vector.quantize_mx(
+                out=codes[0][:, first:last].bitcast(FP8X4),
+                scales=codes[1][:, first:last],
+                in_=grouped[:, first * PACK : last * PACK],
+            )
+
+        def new_grouped():
+            grouped = mid.tile([P, PACK * 512], BF16, name="grouped", align_bytes=64)
+            return grouped
+
+        def new_codes(pool, width, name):
+            words = pool.tile([P, width], U32, name=f"{name}_words", align_bytes=64)
+            scales = pool.tile([P, width], U8, name=f"{name}_bytes", align_bytes=64)
             return words, scales
 
-        def tokens(s):
-            raw = load(xT[s * K_PASS : (s + 1) * K_PASS, :])
-            grouped = group(raw, False)
-            quantise(grouped, token_words[s], token_bytes[s])
+        def list_part(offsets, e):
+            return offsets[:, e * LIST_COLS : (e + 1) * LIST_COLS]
 
-        def gather(e, s):
-            picks = offs_list[:, e * LIST_COLS : (e + 1) * LIST_COLS]
-            nc.vector.tensor_copy(slot_words[e, s][:], token_words[s][:].indirect(picks))
-            nc.vector.tensor_copy(slot_bytes[e, s][:], token_bytes[s][:].indirect(picks))
+        def gather_words(e, s):
+            nc.vector.tensor_copy(slot_words[e, s][:], token_words[s][:].indirect(list_part(offs_list, e)))
 
-        def product(acc, wq, m, words, scales, start, stop):
-            cols = slice(m * P, (m + 1) * P)
+        def gather_plane(e, q):
+            nc.vector.tensor_copy(slot_planes[e, q][:], token_planes[q][:].indirect(list_part(offs_list, e)))
+
+        def product(acc, left, m, right, cols, start, stop):
+            rows = slice(m * P, (m + 1) * P)
             nc.tensor.matmul_mx(
                 out=acc,
-                lhsT=wq[0][:, cols].bitcast(FP8X4),
-                lhsT_scale=wq[1][:, cols],
-                rhs=words.bitcast(FP8X4),
-                rhs_scale=scales,
+                lhsT=left[0][:, rows].bitcast(FP8X4),
+                lhsT_scale=left[1][:, rows],
+                rhs=right[0][:, cols].bitcast(FP8X4),
+                rhs_scale=right[1][:, cols],
                 start=start,
                 stop=stop,
             )
 
-        def project(e, s, banks, wq):
-            for t in range(TILES):
-                product(banks[t][:, 0:C], wq, t, slot_words[e, s][:], slot_bytes[e, s][:], s == 0, s == PASSES - 1)
+        def project(e, s, banks, codes, cols):
+            slots = (slot_words[e, s], slot_planes[e, s // 4][4 * (s % 4) : P])
+            for m in range(SLOT_TILES):
+                product(banks[m][:, 0 : cols.stop - cols.start], slots, m, codes, cols, s == 0, s == PASSES - 1)
 
-        def hidden_rows(w, e, s):
-            return w[e, s * K_PASS : (s + 1) * K_PASS, :]
+        def new_bank():
+            bank = psum.tile([P, 512], F32, name="bank")
+            return bank
 
-        def open_banks():
-            banks = []
-            for t in range(TILES):
-                bank = psum.tile([P, 512], F32, name="bank")
-                banks.append(bank)
-            return banks
+        banks, activated, hidden, turned, h_codes, w2_codes, y_banks, results = {}, {}, {}, {}, {}, {}, {}, {}
 
-        def hidden(e, banks_b, activated):
-            product_h = work.tile([P, TILES, C], F32, name="product_h")
-            for t in range(TILES):
-                nc.vector.tensor_tensor(product_h[:, t, :], activated[:, t, :], banks_b[t][:, 0:C], MULT)
-            grouped = work.tile([P, C * PACK], BF16, name="grouped_h", align_bytes=64)
-            target = grouped[:].rearrange("p (c i j) -> p c j i", i=4, j=PACK)
-            source = product_h[:].rearrange("p j (c i) -> p c j i", i=4)
-            cut = 24
-            nc.scalar.copy(target[:, 0:cut], source[:, 0:cut])
-            nc.vector.tensor_copy(target[:, cut : C // 4], source[:, cut : C // 4])
-            words = work.tile([P, C], U32, name="h_words", align_bytes=64)
-            scales = work.tile([P, C], U8, name="h_bytes", align_bytes=64)
-            nc.vector.quantize_mx(out=words[:].bitcast(FP8X4), scales=scales[:], in_=grouped[:])
-            return words, scales
+        def gelu(e):
+            for m in range(SLOT_TILES):
+                act = work.tile([P, H], F32, name=f"activated{m}")
+                nc.scalar.activation(act[:], banks["w1", e][m][:], GELU)
+                activated[e, m] = act
 
-        def place(e, w2q, words, scales):
-            picks = dst_list[:, e * LIST_COLS : (e + 1) * LIST_COLS]
-            ys = []
-            for half in range(2):
-                bank = psum.tile([P, 512], F32, name="bank")
-                for u in range(2):
-                    product(bank[:, u * C : (u + 1) * C], w2q, 2 * half + u, words[:], scales[:], True, True)
-                for u in range(2):
-                    y = work.tile([P, C], F32, name=f"y{2 * half + u}")
-                    nc.vector.tensor_tensor(y[:], bank[:, u * C : (u + 1) * C], gate_rows[:, e * C : (e + 1) * C], MULT)
-                    ys.append(y)
-            for n in range(N // P):
-                nc.vector.tensor_copy(placed[n][:].indirect(picks), ys[n][:])
+        def multiply(e, m, bank, cols):
+            if (e, m) not in hidden:
+                hidden[e, m] = work.tile([P, H], BF16, name=f"hidden{m}", align_bytes=64)
+            width = cols.stop - cols.start
+            nc.vector.tensor_tensor(hidden[e, m][:, cols], activated[e, m][:, cols], bank[:, 0:width], MULT)
 
-        for e in range(E):
-            banks_a = open_banks()
-            for s in range(PASSES):
-                if e == 0:
-                    tokens(s)
-                    if s == 0:
-                        nc.sync.dma_start(offs_list[:], offs)
-                w1q = weight(hidden_rows(w1, e, s), True, f"w1_{e}{s}")
-                gather(e, s)
-                project(e, s, banks_a, w1q)
-            activated = work.tile([P, TILES, C], F32, name="activated")
-            for t in range(TILES):
-                nc.scalar.activation(activated[:, t, :], banks_a[t][:, 0:C], GELU)
-            banks_b = open_banks()
-            for s in range(PASSES):
-                last = e == E - 1 and s == PASSES - 1
-                if last:
-                    w3q = weight(hidden_rows(w3, e, s), True, f"w3_{e}{s}", cut=44, pieces=4)
+        def turn(e, m):
+            words = hidden[e, m][:].bitcast(F32)
+            turned[e, m] = new_bank()
+            for u in range(2):
+                nc.tensor.transpose(turned[e, m][:, u * P : (u + 1) * P], words[:, u : 2 * P : 2], identity[:])
+
+        def collect(e, on_scalar):
+            grouped_h = work.tile([P, C * PACK], BF16, name="grouped_h", align_bytes=64)
+            pairs = grouped_h[:].bitcast(F32).rearrange("p (m r u) -> p m r u", m=SLOT_TILES, u=2)
+            for m in range(SLOT_TILES):
+                source = turned[e, m][:, 0 : 2 * P].rearrange("p (u r) -> p r u", u=2)
+                if m in on_scalar:
+                    nc.scalar.copy(pairs[:, m], source)
                 else:
-                    w3q = weight(hidden_rows(w3, e, s), True, f"w3_{e}{s}")
-                project(e, s, banks_b, w3q)
-            if e == 0:
+                    nc.vector.tensor_copy(pairs[:, m], source)
+            h_codes[e] = (new_codes(work, C, "h"), grouped_h)
+
+        def quantise_h(e):
+            quantise(h_codes[e][0], h_codes[e][1], 0, C)
+
+        def down(e, n):
+            y_banks[e, n] = new_bank()
+            product(y_banks[e, n][:, 0:C], w2_codes[e], n, h_codes[e][0], slice(0, C), True, True)
+
+        def leave(e, n):
+            y = work.tile([P, C], F32, name=f"y{n}")
+            results[e, n] = y
+            if CFG["fused"][e][n] == 1:
+                nc.scalar.copy(y[:], y_banks[e, n][:, 0:C])
+            else:
+                nc.vector.tensor_tensor(y[:], y_banks[e, n][:, 0:C], gate_rows[:, e * C : (e + 1) * C], MULT)
+
+        def scatter(e, n):
+            where = placed[n][:].indirect(list_part(dst_list, e))
+            if CFG["fused"][e][n] == 1:
+                nc.vector.tensor_tensor(where, results[e, n][:], gate_rows[:, e * C : (e + 1) * C], MULT)
+            else:
+                nc.vector.tensor_copy(where, results[e, n][:])
+
+        whole = slice(0, 512)
+        halves = (slice(0, 256), slice(256, 512))
+        parts = (slice(0, 256), slice(256, 512), slice(0, 512))
+        stream = list(CFG["stream"])
+        source = {"w1": w1, "w3": w3}
+
+        def rows_of(kind, e, s):
+            rows = slice(s * K_PASS, (s + 1) * K_PASS)
+            if kind == "x":
+                return xT[rows, :]
+            return source[kind][e, rows, :]
+
+        def finish(kind, e, s, grouped):
+            if kind == "x":
+                quantise((token_words[s], token_planes[s // 4][4 * (s % 4) : P]), grouped)
+                return
+            if kind == "w2":
+                quantise(w2_codes[0], grouped, parts[s].start, parts[s].stop)
+                return
+            codes = new_codes(keep, 512, f"{kind}_{e}{s}")
+            quantise(codes, grouped)
+            if kind == "w3" and e == E - 1:
+                if s == 0:
+                    banks[kind, e] = [[new_bank() for m in range(SLOT_TILES)] for h in range(2)]
+                for h in range(2):
+                    project(e, s, banks[kind, e][h], codes, halves[h])
+                return
+            if s == 0:
+                banks[kind, e] = [new_bank() for m in range(SLOT_TILES)]
+            project(e, s, banks[kind, e], codes, whole)
+
+        def run(job):
+            what, e, n = job
+            if what == "gw":
+                gather_words(e, n)
+            elif what == "gp":
+                gather_plane(e, n)
+            elif what == "gelu":
+                gelu(e)
+            elif what == "hid":
+                for m in range(SLOT_TILES):
+                    multiply(0, m, banks["w3", 0][m], whole)
+                    turn(0, m)
+            elif what == "col":
+                collect(0, CFG["col0"])
+            elif what == "qh":
+                quantise_h(0)
+            elif what == "down":
+                down(0, n)
+            elif what == "leave":
+                leave(0, n)
+            else:
+                scatter(0, n)
+
+        w2_codes[0] = new_codes(keep, 512, "w2_first")
+        before = None
+        for step, (kind, e, s) in enumerate(stream):
+            if kind == "w2":
+                raw = stage.tile([P, PACK, 512], F32, name="raw")
+                nc.sync.dma_start(out=raw[:, :, parts[s]], in_=w2[0].rearrange("(p j) w -> p j w", j=PACK)[:, :, parts[s]])
+            else:
+                raw = load(rows_of(kind, e, s), CFG["x0"] if step == 0 else 1)
+            if step == 0:
+                nc.sync.dma_start(offs_list[:], offs)
+            if step == CFG["lists"]:
                 nc.sync.dma_start(dst_list[:], dst)
                 nc.sync.dma_start(gate_rows[:], gate[0:P, :])
-            w2q = weight(w2[e], False, f"w2_{e}")
-            h_words, h_bytes = hidden(e, banks_b, activated)
-            place(e, w2q, h_words, h_bytes)
+            grouped = new_grouped()
+            if step == 0:
+                w = 128 // CFG["x0"]
+                for q in range(CFG["x0"]):
+                    interleave(grouped, raw, q * w, q * w + CFG["share"][0] // CFG["x0"], q * w + w)
+            elif kind == "w2":
+                interleave(grouped, raw, parts[s].start // 4, parts[s].start // 4 + CFG["share"][step], parts[s].stop // 4)
+            else:
+                interleave(grouped, raw, 0, CFG["share"][step], 128)
+            if before is not None:
+                finish(*before)
+            for at, job in CFG["jobs"]:
+                if at == step:
+                    run(job)
+            before = (kind, e, s, grouped)
+
+        last = E - 1
+        raw = load(rows_of("w3", last, PASSES - 1), 2)
+        raw_w2 = load(w2[last])
+        grouped_w2 = keep.tile([P, PACK * 512], BF16, name="grouped_w2", align_bytes=64)
+        codes = new_codes(keep, 512, "w3_final")
+        w2_codes[last] = new_codes(keep, 512, "w2_final")
+        for h in range(2):
+            grouped = new_grouped()
+            interleave(grouped, raw, 64 * h, 64 * h + CFG["cut"][h], 64 * h + 64)
+            if h == 0:
+                finish(*before)
+            quantise(codes, grouped, 256 * h, 256 * h + 256)
+            project(last, PASSES - 1, banks["w3", last][h], codes, halves[h])
+        for h in range(2):
+            interleave(grouped_w2, raw_w2, 64 * h, 64 * h + CFG["cut"][2 + h], 64 * h + 64)
+        for m in range(SLOT_TILES):
+            for h in range(2):
+                multiply(last, m, banks["w3", last][h][m], halves[h])
+            turn(last, m)
+        collect(last, CFG["col1"])
+        quantise_h(last)
+        for h in range(2):
+            quantise(w2_codes[last], grouped_w2, 256 * h, 256 * h + 256)
+            for n in (2 * h, 2 * h + 1):
+                down(last, n)
+                leave(last, n)
         for n in range(N // P):
+            scatter(last, n)
             nc.sync.dma_start(out[n * P : (n + 1) * P, :], placed[n][:])

@@ -15,7 +15,7 @@ LIST_COLS = C // 16
 FLOPS = 2 * E * C * (2 * K * H + H * N)
 BYTES = 4 * (K * T + 2 * E * K * H + E * H * N + E * C + N * T) + 2 * 2 * P * E * LIST_COLS
 
-CFG = {'stage': 10, 'mid': 4, 'lists': 12, 'x0': 2, 'share': [88, 88, 88, 88, 88, 88, 88, 88, 88, 88, 88, 88, 88, 64, 0, 88, 88, 64, 128, 100, 128, 128, 0, 0, 100], 'cut': [64, 30, 64, 64], 'col0': [0], 'col1': [], 'fused': [[0, 1, 0, 1], [1, 1, 1, 1]], 'jobs': [(3, ('gw', 0, 0)), (4, ('gw', 0, 1)), (5, ('gw', 0, 2)), (6, ('gw', 0, 3)), (7, ('gw', 0, 4)), (5, ('gp', 0, 0)), (7, ('gp', 0, 1)), (8, ('gw', 1, 0)), (9, ('gw', 1, 1)), (10, ('gw', 1, 2)), (11, ('gw', 1, 3)), (12, ('gw', 1, 4)), (13, ('gp', 1, 0)), (14, ('gp', 1, 1)), (12, ('gelu', 0, 0)), (16, ('hid', 0, 0)), (17, ('col', 0, 0)), (18, ('qh', 0, 0)), (18, ('down', 0, 0)), (18, ('leave', 0, 0)), (19, ('sc', 0, 0)), (18, ('down', 0, 1)), (18, ('leave', 0, 1)), (19, ('sc', 0, 1)), (18, ('down', 0, 2)), (18, ('leave', 0, 2)), (19, ('sc', 0, 2)), (18, ('down', 0, 3)), (18, ('leave', 0, 3)), (19, ('sc', 0, 3)), (23, ('gelu', 1, 0))], 'stream': [('x', 0, 0), ('x', 0, 1), ('x', 0, 2), ('x', 0, 3), ('x', 0, 4), ('w1', 0, 0), ('w1', 0, 1), ('w1', 0, 2), ('w1', 0, 3), ('w1', 0, 4), ('w3', 0, 0), ('w3', 0, 1), ('w3', 0, 2), ('w3', 0, 3), ('w3', 0, 4), ('w1', 1, 0), ('w2', 0, 2), ('w1', 1, 1), ('w1', 1, 2), ('w1', 1, 3), ('w1', 1, 4), ('w3', 1, 0), ('w3', 1, 1), ('w3', 1, 2), ('w3', 1, 3)]}
+CFG = {'stage': 12, 'mid': 4, 'lists': 12, 'x0': 2, 'share': [88, 88, 88, 88, 88, 88, 88, 88, 88, 88, 88, 88, 88, 64, 0, 88, 88, 64, 128, 100, 128, 128, 0, 0, 100], 'cut': [64, 30, 64, 64], 'col0': [0], 'col1': [], 'fused': [[0, 0, 0, 0], [0, 0, 0, 0]], 'jobs': [(3, ('gw', 0, 0)), (4, ('gw', 0, 1)), (5, ('gw', 0, 2)), (6, ('gw', 0, 3)), (7, ('gw', 0, 4)), (5, ('gp', 0, 0)), (7, ('gp', 0, 1)), (8, ('gw', 1, 0)), (9, ('gw', 1, 1)), (10, ('gw', 1, 2)), (11, ('gw', 1, 3)), (12, ('gw', 1, 4)), (13, ('gp', 1, 0)), (14, ('gp', 1, 1)), (12, ('gelu', 0, 0)), (16, ('hid', 0, 0)), (17, ('col', 0, 0)), (18, ('qh', 0, 0)), (18, ('down', 0, 0)), (18, ('leave', 0, 0)), (19, ('sc', 0, 0)), (18, ('down', 0, 1)), (18, ('leave', 0, 1)), (19, ('sc', 0, 1)), (18, ('down', 0, 2)), (18, ('leave', 0, 2)), (19, ('sc', 0, 2)), (18, ('down', 0, 3)), (18, ('leave', 0, 3)), (19, ('sc', 0, 3)), (23, ('gelu', 1, 0))], 'stream': [('x', 0, 0), ('x', 0, 1), ('x', 0, 2), ('x', 0, 3), ('x', 0, 4), ('w1', 0, 0), ('w1', 0, 1), ('w1', 0, 2), ('w1', 0, 3), ('w1', 0, 4), ('w3', 0, 0), ('w3', 0, 1), ('w3', 0, 2), ('w3', 0, 3), ('w3', 0, 4), ('w1', 1, 0), ('w2', 0, 2), ('w1', 1, 1), ('w1', 1, 2), ('w1', 1, 3), ('w1', 1, 4), ('w3', 1, 0), ('w3', 1, 1), ('w3', 1, 2), ('w3', 1, 3)]}
 
 F32 = mybir.dt.float32
 BF16 = mybir.dt.bfloat16

@@ -15,7 +15,7 @@ LIST_COLS = C // 16
 FLOPS = 2 * E * C * (2 * K * H + H * N)
 BYTES = 4 * (K * T + 2 * E * K * H + E * H * N + E * C + N * T) + 2 * 2 * P * E * LIST_COLS
 
-CFG = {'stage': 12, 'mid': 4, 'lists': 12, 'x0': 2, 'share': [88, 88, 88, 88, 88, 88, 88, 88, 88, 88, 88, 88, 88, 64, 0, 88, 88, 64, 128, 100, 128, 128, 0, 0, 100], 'cut': [64, 30, 64, 64], 'col0': [0], 'col1': [], 'fused': [[0, 0, 0, 0], [0, 0, 0, 0]], 'jobs': [(3, ('gw', 0, 0)), (4, ('gw', 0, 1)), (5, ('gw', 0, 2)), (6, ('gw', 0, 3)), (7, ('gw', 0, 4)), (5, ('gp', 0, 0)), (7, ('gp', 0, 1)), (8, ('gw', 1, 0)), (9, ('gw', 1, 1)), (10, ('gw', 1, 2)), (11, ('gw', 1, 3)), (12, ('gw', 1, 4)), (13, ('gp', 1, 0)), (14, ('gp', 1, 1)), (12, ('gelu', 0, 0)), (16, ('hid', 0, 0)), (17, ('col', 0, 0)), (18, ('qh', 0, 0)), (18, ('down', 0, 0)), (18, ('leave', 0, 0)), (19, ('sc', 0, 0)), (18, ('down', 0, 1)), (18, ('leave', 0, 1)), (19, ('sc', 0, 1)), (18, ('down', 0, 2)), (18, ('leave', 0, 2)), (19, ('sc', 0, 2)), (18, ('down', 0, 3)), (18, ('leave', 0, 3)), (19, ('sc', 0, 3)), (23, ('gelu', 1, 0))], 'stream': [('x', 0, 0), ('x', 0, 1), ('x', 0, 2), ('x', 0, 3), ('x', 0, 4), ('w1', 0, 0), ('w1', 0, 1), ('w1', 0, 2), ('w1', 0, 3), ('w1', 0, 4), ('w3', 0, 0), ('w3', 0, 1), ('w3', 0, 2), ('w3', 0, 3), ('w3', 0, 4), ('w1', 1, 0), ('w2', 0, 2), ('w1', 1, 1), ('w1', 1, 2), ('w1', 1, 3), ('w1', 1, 4), ('w3', 1, 0), ('w3', 1, 1), ('w3', 1, 2), ('w3', 1, 3)]}
+CFG = {'stage': 10, 'mid': 4, 'lists': 12, 'x0': 2, 'share': [88, 88, 88, 88, 88, 88, 88, 88, 88, 88, 88, 88, 88, 64, 0, 88, 88, 64, 128, 100, 128, 128, 0, 0, 100], 'cut': [64, 30, 64, 64], 'col0': [0], 'col1': [], 'fused': [[0, 1, 0, 1], [0, 1, 1, 1]], 'jobs': [(3, ('gw', 0, 0)), (4, ('gw', 0, 1)), (5, ('gw', 0, 2)), (6, ('gw', 0, 3)), (7, ('gw', 0, 4)), (5, ('gp', 0, 0)), (7, ('gp', 0, 1)), (8, ('gw', 1, 0)), (9, ('gw', 1, 1)), (10, ('gw', 1, 2)), (11, ('gw', 1, 3)), (12, ('gw', 1, 4)), (13, ('gp', 1, 0)), (14, ('gp', 1, 1)), (12, ('gelu', 0, 0)), (16, ('hid', 0, 0)), (17, ('col', 0, 0)), (18, ('qh', 0, 0)), (18, ('down', 0, 0)), (18, ('leave', 0, 0)), (19, ('sc', 0, 0)), (18, ('down', 0, 1)), (18, ('leave', 0, 1)), (19, ('sc', 0, 1)), (18, ('down', 0, 2)), (18, ('leave', 0, 2)), (19, ('sc', 0, 2)), (18, ('down', 0, 3)), (18, ('leave', 0, 3)), (19, ('sc', 0, 3)), (23, ('gelu', 1, 0))], 'stream': [('x', 0, 0), ('x', 0, 1), ('x', 0, 2), ('x', 0, 3), ('x', 0, 4), ('w1', 0, 0), ('w1', 0, 1), ('w1', 0, 2), ('w1', 0, 3), ('w1', 0, 4), ('w3', 0, 0), ('w3', 0, 1), ('w3', 0, 2), ('w3', 0, 3), ('w3', 0, 4), ('w1', 1, 0), ('w2', 0, 2), ('w1', 1, 1), ('w1', 1, 2), ('w1', 1, 3), ('w1', 1, 4), ('w3', 1, 0), ('w3', 1, 1), ('w3', 1, 2), ('w3', 1, 3)], 'w2p': 2}
 
 F32 = mybir.dt.float32
 BF16 = mybir.dt.bfloat16
@@ -38,7 +38,7 @@ def tile_moe_two_glu_gelu_kernel(tc, xT, w1, w3, w2, gate, offs, dst, out):
 
         offs_list = keep.tile([P, E * LIST_COLS], U16, name="offs_list")
         dst_list = keep.tile([P, E * LIST_COLS], U16, name="dst_list")
-        gate_rows = keep.tile([P, E * C], F32, name="gate_rows")
+        gate_rows = [keep.tile([P, C], F32, name=f"gate_rows{e}") for e in range(E)]
         warm = keep.tile([P, 8], F32, name="warm")
         nc.vector.memset(warm[:], 0.0)
         nc.scalar.activation(warm[:], warm[:], GELU)
@@ -165,12 +165,12 @@ def tile_moe_two_glu_gelu_kernel(tc, xT, w1, w3, w2, gate, offs, dst, out):
             if CFG["fused"][e][n] == 1:
                 nc.scalar.copy(y[:], y_banks[e, n][:, 0:C])
             else:
-                nc.vector.tensor_tensor(y[:], y_banks[e, n][:, 0:C], gate_rows[:, e * C : (e + 1) * C], MULT)
+                nc.vector.tensor_tensor(y[:], y_banks[e, n][:, 0:C], gate_rows[e][:], MULT)
 
         def scatter(e, n):
             where = placed[n][:].indirect(list_part(dst_list, e))
             if CFG["fused"][e][n] == 1:
-                nc.vector.tensor_tensor(where, results[e, n][:], gate_rows[:, e * C : (e + 1) * C], MULT)
+                nc.vector.tensor_tensor(where, results[e, n][:], gate_rows[e][:], MULT)
             else:
                 nc.vector.tensor_copy(where, results[e, n][:])
 
@@ -240,7 +240,7 @@ def tile_moe_two_glu_gelu_kernel(tc, xT, w1, w3, w2, gate, offs, dst, out):
                 nc.sync.dma_start(offs_list[:], offs)
             if step == CFG["lists"]:
                 nc.sync.dma_start(dst_list[:], dst)
-                nc.sync.dma_start(gate_rows[:], gate[0:P, :])
+                nc.sync.dma_start(gate_rows[0][:], gate[0:P, 0:C])
             grouped = new_grouped()
             if step == 0:
                 w = 128 // CFG["x0"]
@@ -259,7 +259,8 @@ def tile_moe_two_glu_gelu_kernel(tc, xT, w1, w3, w2, gate, offs, dst, out):
 
         last = E - 1
         raw = load(rows_of("w3", last, PASSES - 1), 2)
-        raw_w2 = load(w2[last])
+        nc.sync.dma_start(gate_rows[last][:], gate[0:P, C : 2 * C])
+        raw_w2 = load(w2[last], CFG.get("w2p", 1))
         grouped_w2 = keep.tile([P, PACK * 512], BF16, name="grouped_w2", align_bytes=64)
         codes = new_codes(keep, 512, "w3_final")
         w2_codes[last] = new_codes(keep, 512, "w2_final")

from contextlib import ExitStack

import concourse.mybir as mybir
from concourse.masks import make_identity

K, T, E, C, H, N = 2560, 512, 2, 256, 512, 512
P = 128
PACK = 4
K_PASS = P * PACK
PASSES = K // K_PASS
PLANES = 2
SLOT_TILES = C // P
LIST_COLS = C // 16

FLOPS = 2 * E * C * (2 * K * H + H * N)
BYTES = 4 * (K * T + 2 * E * K * H + E * H * N + E * C + N * T) + 2 * 2 * P * E * LIST_COLS

CFG = {'stage': 10, 'mid': 4, 'lists': 12, 'x0': 2, 'share': [88, 88, 88, 88, 88, 88, 88, 88, 88, 88, 88, 88, 88, 64, 0, 88, 88, 64, 128, 100, 128, 128, 0, 0, 100], 'cut': [64, 30, 64, 64], 'col0': [0], 'col1': [], 'fused': [[0, 1, 0, 1], [0, 1, 1, 1]], 'jobs': [(3, ('gw', 0, 0)), (4, ('gw', 0, 1)), (5, ('gw', 0, 2)), (6, ('gw', 0, 3)), (7, ('gw', 0, 4)), (5, ('gp', 0, 0)), (7, ('gp', 0, 1)), (8, ('gw', 1, 0)), (9, ('gw', 1, 1)), (10, ('gw', 1, 2)), (11, ('gw', 1, 3)), (12, ('gw', 1, 4)), (13, ('gp', 1, 0)), (14, ('gp', 1, 1)), (12, ('gelu', 0, 0)), (16, ('hid', 0, 0)), (17, ('col', 0, 0)), (18, ('qh', 0, 0)), (18, ('down', 0, 0)), (18, ('leave', 0, 0)), (19, ('sc', 0, 0)), (18, ('down', 0, 1)), (18, ('leave', 0, 1)), (19, ('sc', 0, 1)), (18, ('down', 0, 2)), (18, ('leave', 0, 2)), (19, ('sc', 0, 2)), (18, ('down', 0, 3)), (18, ('leave', 0, 3)), (19, ('sc', 0, 3)), (23, ('gelu', 1, 0))], 'stream': [('x', 0, 0), ('x', 0, 1), ('x', 0, 2), ('x', 0, 3), ('x', 0, 4), ('w1', 0, 0), ('w1', 0, 1), ('w1', 0, 2), ('w1', 0, 3), ('w1', 0, 4), ('w3', 0, 0), ('w3', 0, 1), ('w3', 0, 2), ('w3', 0, 3), ('w3', 0, 4), ('w1', 1, 0), ('w2', 0, 2), ('w1', 1, 1), ('w1', 1, 2), ('w1', 1, 3), ('w1', 1, 4), ('w3', 1, 0), ('w3', 1, 1), ('w3', 1, 2), ('w3', 1, 3)], 'w2p': 2}

F32 = mybir.dt.float32
BF16 = mybir.dt.bfloat16
U32 = mybir.dt.uint32
U16 = mybir.dt.uint16
U8 = mybir.dt.uint8
FP8X4 = mybir.dt.float8_e4m3fn_x4
GELU = mybir.ActivationFunctionType.Gelu_apprx_tanh
MULT = mybir.AluOpType.mult


def tile_moe_two_glu_gelu_kernel(tc, xT, w1, w3, w2, gate, offs, dst, out):
    nc = tc.nc
    with ExitStack() as ctx:
        keep = ctx.enter_context(tc.tile_pool(name="keep", bufs=1))
        stage = ctx.enter_context(tc.tile_pool(name="stage", bufs=CFG["stage"]))
        mid = ctx.enter_context(tc.tile_pool(name="mid", bufs=CFG["mid"]))
        work = ctx.enter_context(tc.tile_pool(name="work", bufs=2))
        psum = ctx.enter_context(tc.psum_pool(name="psum", bufs=8))

        offs_list = keep.tile([P, E * LIST_COLS], U16, name="offs_list")
        dst_list = keep.tile([P, E * LIST_COLS], U16, name="dst_list")
        gate_rows = [keep.tile([P, C], F32, name=f"gate_rows{e}") for e in range(E)]
        warm = keep.tile([P, 8], F32, name="warm")
        nc.vector.memset(warm[:], 0.0)
        nc.scalar.activation(warm[:], warm[:], GELU)
        identity = keep.tile([P, P], F32, name="identity")
        make_identity(nc, identity[:])

        token_words = [keep.tile([P, T], U32, name=f"token_words{s}", align_bytes=64) for s in range(PASSES)]
        token_planes = [keep.tile([P, T], U8, name=f"token_planes{q}", align_bytes=64) for q in range(PLANES)]
        for plane in token_planes:
            nc.gpsimd.memset(plane[:], 0)
        slot_words = {}
        slot_planes = {}
        for e in range(E):
            for s in range(PASSES):
                slot_words[e, s] = keep.tile([P, C], U32, name=f"slot_words{e}{s}", align_bytes=64)
            for q in range(PLANES):
                slot_planes[e, q] = keep.tile([P, C], U8, name=f"slot_planes{e}{q}", align_bytes=64)
        placed = [keep.tile([P, T], F32, name=f"placed{n}") for n in range(N // P)]

        def load(rows, pieces=1):
            raw = stage.tile([P, PACK, 512], F32, name="raw")
            view = rows.rearrange("(p j) w -> p j w", j=PACK)
            width = 512 // pieces
            for q in range(pieces):
                cols = slice(q * width, (q + 1) * width)
                nc.sync.dma_start(out=raw[:, :, cols], in_=view[:, :, cols])
            return raw

        def interleave(grouped, raw, first, cut, last):
            target = grouped[:].rearrange("p (c i j) -> p c j i", i=4, j=PACK)
            source = raw[:].rearrange("p j (c i) -> p c j i", i=4)
            if cut > first:
                nc.scalar.copy(target[:, first:cut], source[:, first:cut])
            if last > cut:
                nc.vector.tensor_copy(target[:, cut:last], source[:, cut:last])

        def quantise(codes, grouped, first=0, last=512):
            nc.vector.quantize_mx(
                out=codes[0][:, first:last].bitcast(FP8X4),
                scales=codes[1][:, first:last],
                in_=grouped[:, first * PACK : last * PACK],
            )

        def new_grouped():
            grouped = mid.tile([P, PACK * 512], BF16, name="grouped", align_bytes=64)
            return grouped

        def new_codes(pool, width, name):
            words = pool.tile([P, width], U32, name=f"{name}_words", align_bytes=64)
            scales = pool.tile([P, width], U8, name=f"{name}_bytes", align_bytes=64)
            return words, scales

        def list_part(offsets, e):
            return offsets[:, e * LIST_COLS : (e + 1) * LIST_COLS]

        def gather_words(e, s):
            nc.vector.tensor_copy(slot_words[e, s][:], token_words[s][:].indirect(list_part(offs_list, e)))

        def gather_plane(e, q):
            nc.vector.tensor_copy(slot_planes[e, q][:], token_planes[q][:].indirect(list_part(offs_list, e)))

        def product(acc, left, m, right, cols, start, stop):
            rows = slice(m * P, (m + 1) * P)
            nc.tensor.matmul_mx(
                out=acc,
                lhsT=left[0][:, rows].bitcast(FP8X4),
                lhsT_scale=left[1][:, rows],
                rhs=right[0][:, cols].bitcast(FP8X4),
                rhs_scale=right[1][:, cols],
                start=start,
                stop=stop,
            )

        def project(e, s, banks, codes, cols):
            slots = (slot_words[e, s], slot_planes[e, s // 4][4 * (s % 4) : P])
            for m in range(SLOT_TILES):
                product(banks[m][:, 0 : cols.stop - cols.start], slots, m, codes, cols, s == 0, s == PASSES - 1)

        def new_bank():
            bank = psum.tile([P, 512], F32, name="bank")
            return bank

        banks, activated, hidden, turned, h_codes, w2_codes, y_banks, results = {}, {}, {}, {}, {}, {}, {}, {}

        def gelu(e):
            for m in range(SLOT_TILES):
                act = work.tile([P, H], F32, name=f"activated{m}")
                nc.scalar.activation(act[:], banks["w1", e][m][:], GELU)
                activated[e, m] = act

        def multiply(e, m, bank, cols):
            if (e, m) not in hidden:
                hidden[e, m] = work.tile([P, H], BF16, name=f"hidden{m}", align_bytes=64)
            width = cols.stop - cols.start
            nc.vector.tensor_tensor(hidden[e, m][:, cols], activated[e, m][:, cols], bank[:, 0:width], MULT)

        def turn(e, m):
            words = hidden[e, m][:].bitcast(F32)
            turned[e, m] = new_bank()
            for u in range(2):
                nc.tensor.transpose(turned[e, m][:, u * P : (u + 1) * P], words[:, u : 2 * P : 2], identity[:])

        def collect(e, on_scalar):
            grouped_h = work.tile([P, C * PACK], BF16, name="grouped_h", align_bytes=64)
            pairs = grouped_h[:].bitcast(F32).rearrange("p (m r u) -> p m r u", m=SLOT_TILES, u=2)
            for m in range(SLOT_TILES):
                source = turned[e, m][:, 0 : 2 * P].rearrange("p (u r) -> p r u", u=2)
                if m in on_scalar:
                    nc.scalar.copy(pairs[:, m], source)
                else:
                    nc.vector.tensor_copy(pairs[:, m], source)
            h_codes[e] = (new_codes(work, C, "h"), grouped_h)

        def quantise_h(e):
            quantise(h_codes[e][0], h_codes[e][1], 0, C)

        def down(e, n):
            y_banks[e, n] = new_bank()
            product(y_banks[e, n][:, 0:C], w2_codes[e], n, h_codes[e][0], slice(0, C), True, True)

        def leave(e, n):
            y = work.tile([P, C], F32, name=f"y{n}")
            results[e, n] = y
            if CFG["fused"][e][n] == 1:
                nc.scalar.copy(y[:], y_banks[e, n][:, 0:C])
            else:
                nc.vector.tensor_tensor(y[:], y_banks[e, n][:, 0:C], gate_rows[e][:], MULT)

        def scatter(e, n):
            where = placed[n][:].indirect(list_part(dst_list, e))
            if CFG["fused"][e][n] == 1:
                nc.vector.tensor_tensor(where, results[e, n][:], gate_rows[e][:], MULT)
            else:
                nc.vector.tensor_copy(where, results[e, n][:])

        whole = slice(0, 512)
        halves = (slice(0, 256), slice(256, 512))
        parts = (slice(0, 256), slice(256, 512), slice(0, 512))
        stream = list(CFG["stream"])
        source = {"w1": w1, "w3": w3}

        def rows_of(kind, e, s):
            rows = slice(s * K_PASS, (s + 1) * K_PASS)
            if kind == "x":
                return xT[rows, :]
            return source[kind][e, rows, :]

        def finish(kind, e, s, grouped):
            if kind == "x":
                quantise((token_words[s], token_planes[s // 4][4 * (s % 4) : P]), grouped)
                return
            if kind == "w2":
                quantise(w2_codes[0], grouped, parts[s].start, parts[s].stop)
                return
            codes = new_codes(keep, 512, f"{kind}_{e}{s}")
            quantise(codes, grouped)
            if kind == "w3" and e == E - 1:
                if s == 0:
                    banks[kind, e] = [[new_bank() for m in range(SLOT_TILES)] for h in range(2)]
                for h in range(2):
                    project(e, s, banks[kind, e][h], codes, halves[h])
                return
            if s == 0:
                banks[kind, e] = [new_bank() for m in range(SLOT_TILES)]
            project(e, s, banks[kind, e], codes, whole)

        def run(job):
            what, e, n = job
            if what == "gw":
                gather_words(e, n)
            elif what == "gp":
                gather_plane(e, n)
            elif what == "gelu":
                gelu(e)
            elif what == "hid":
                for m in range(SLOT_TILES):
                    multiply(0, m, banks["w3", 0][m], whole)
                    turn(0, m)
            elif what == "col":
                collect(0, CFG["col0"])
            elif what == "qh":
                quantise_h(0)
            elif what == "down":
                down(0, n)
            elif what == "leave":
                leave(0, n)
            else:
                scatter(0, n)

        w2_codes[0] = new_codes(keep, 512, "w2_first")
        before = None
        for step, (kind, e, s) in enumerate(stream):
            if kind == "w2":
                raw = stage.tile([P, PACK, 512], F32, name="raw")
                nc.sync.dma_start(out=raw[:, :, parts[s]], in_=w2[0].rearrange("(p j) w -> p j w", j=PACK)[:, :, parts[s]])
            else:
                raw = load(rows_of(kind, e, s), CFG["x0"] if step == 0 else 1)
            if step == 0:
                nc.sync.dma_start(offs_list[:], offs)
            if step == CFG["lists"]:
                nc.sync.dma_start(dst_list[:], dst)
                nc.sync.dma_start(gate_rows[0][:], gate[0:P, 0:C])
            grouped = new_grouped()
            if step == 0:
                w = 128 // CFG["x0"]
                for q in range(CFG["x0"]):
                    interleave(grouped, raw, q * w, q * w + CFG["share"][0] // CFG["x0"], q * w + w)
            elif kind == "w2":
                interleave(grouped, raw, parts[s].start // 4, parts[s].start // 4 + CFG["share"][step], parts[s].stop // 4)
            else:
                interleave(grouped, raw, 0, CFG["share"][step], 128)
            if before is not None:
                finish(*before)
            for at, job in CFG["jobs"]:
                if at == step:
                    run(job)
            before = (kind, e, s, grouped)

        last = E - 1
        raw = load(rows_of("w3", last, PASSES - 1), 2)
        nc.sync.dma_start(gate_rows[last][:], gate[0:P, C : 2 * C])
        raw_w2 = load(w2[last], CFG.get("w2p", 1))
        grouped_w2 = keep.tile([P, PACK * 512], BF16, name="grouped_w2", align_bytes=64)
        codes = new_codes(keep, 512, "w3_final")
        w2_codes[last] = new_codes(keep, 512, "w2_final")
        for h in range(2):
            grouped = new_grouped()
            interleave(grouped, raw, 64 * h, 64 * h + CFG["cut"][h], 64 * h + 64)
            if h == 0:
                finish(*before)
            quantise(codes, grouped, 256 * h, 256 * h + 256)
            project(last, PASSES - 1, banks["w3", last][h], codes, halves[h])
        for h in range(2):
            interleave(grouped_w2, raw_w2, 64 * h, 64 * h + CFG["cut"][2 + h], 64 * h + 64)
        for m in range(SLOT_TILES):
            for h in range(2):
                multiply(last, m, banks["w3", last][h][m], halves[h])
            turn(last, m)
        collect(last, CFG["col1"])
        quantise_h(last)
        for h in range(2):
            quantise(w2_codes[last], grouped_w2, 256 * h, 256 * h + 256)
            for n in (2 * h, 2 * h + 1):
                down(last, n)
                leave(last, n)
        for n in range(N // P):
            scatter(last, n)
            nc.sync.dma_start(out[n * P : (n + 1) * P, :], placed[n][:])
